import numpy as np, ml_dtypes
CORES = [13,21,141,149]
N = 4
import mx_ref
NC, G = 128, 2
C = np.float32(0.019)
BF = ml_dtypes.bfloat16
def cut(t, i, w=512):
    return t[:, w * i:w * i + w]
def tile(rs):
    return np.stack(rs, axis=2).reshape(128, -1).astype(BF)
def layer(w, X):
    out = []
    for i in range(G):
        for t in range(len(X)):
            p = mx_ref.matmul(mx_ref.quantize(cut(w, len(X) * i + t)), X[t])
            z = p if t == 0 else z + p
        out.append(z)
    return out
def act(Z):
    return [np.maximum(s * z, 0) * C for z in Z for s in (1, -1)]
def pick(b):
    s = np.zeros((128, 128, 4), np.float32)
    s[np.arange(128), np.arange(128), b] = 1.0
    return mx_ref.quantize(s.reshape(128, 512).astype(BF))
def setup_inputs(rng):
    def f(*shape):
        return mx_ref.flush((rng.standard_normal(shape, dtype=np.float32) * np.exp2(rng.integers(-2, 3, shape[:-1] + (1,)))).astype(BF))
    return {"a": f(N, 128, G * 512), "b": f(N, 128, N * 4 * NC), "gr": f(N, 128, N * 4 * NC)}
def setup_inputs_blocks(rng):
    d = setup_inputs(rng)
    for k in ("a", "b", "gr"): d[k] = mx_ref.spread(d[k], rng, 2)
    return d
def setup_inputs_wide(rng):
    d = setup_inputs(rng)
    for k in ("a", "b", "gr"): d[k] = mx_ref.flush((d[k].astype(np.float32) * np.exp2(rng.integers(-4, 5, (N, 1, 1))).astype(np.float32)).astype(BF))
    return d
def setup_inputs_zeros(rng):
    d = setup_inputs(rng); v = d["b"].reshape(N, 128, -1, 4).copy()
    v[np.broadcast_to((rng.random((N, 1, v.shape[2], 1)) < 0.33), v.shape)] = 0
    d["b"] = v.reshape(d["b"].shape)
    return d
def reference(a, b, gr):
    S = [pick(t) for t in range(4)]
    held = lambda q: [mx_ref.matmul(S[t], q) for t in range(4)]
    y = np.zeros((N, 128, NC, 4), np.float32); e = np.zeros((N, N, 128, NC, 4), np.float32)
    for c in range(N):
        for r in range(N):
            R = act(layer(a[r], [mx_ref.quantize(cut(b[r], c, 4 * NC))])); q = mx_ref.quantize(tile(R))
            D = held(q)
            e[r, c] = np.stack([R[t] - D[t] for t in range(4)], axis=2)
            p = np.stack(D if r == c else held(q), axis=2)
            q2 = mx_ref.quantize((cut(gr[r], c, 4 * NC).astype(np.float32) + e[r, c].reshape(128, -1)).astype(BF))
            p = p + np.stack(held(q2), axis=2)
            y[c] = p if r == 0 else y[c] + p
    return {"y": y.reshape(N, 128, 4 * NC)}

import numpy as np
from concourse.bass import DstId, RemoteDMATransfer
from concourse.mybir import dt, AluOpType, ActivationFunctionType

X4 = "float8_e4m3fn_x4"
SCRATCH = {
    "ab": ("sbuf", [128, 1024], "bfloat16"),
    "bb": ("sbuf", [128, 2048], "bfloat16"),
    "gb": ("sbuf", [128, 2048], "bfloat16"),
    "w": ("sbuf", [128, 516], "bfloat16"),
    "h": ("sbuf", [128, 2048], "bfloat16"),
    "u": ("sbuf", [128, 2048], "bfloat16"),
    "rf": ("sbuf", [128, 2048], "float32"),
    "ow": ("sbuf", [128, 512], "float32"),
    "ys": ("sbuf", [128, 512], "float32"),
    "ac": ("sbuf", [128, 256], X4), "ap": ("sbuf", [128, 256], "uint8"),
    "bc": ("sbuf", [128, 512], X4), "bp": ("sbuf", [128, 512], "uint8"),
    "sc": ("sbuf", [128, 512], X4), "sp": ("sbuf", [128, 512], "uint8"),
    "tc": ("sbuf", [128, 1024], X4), "tp": ("sbuf", [128, 1024], "uint8"),
    "lc": ("sbuf", [128, 1024], X4), "lp": ("sbuf", [128, 1024], "uint8"),
    "hc": ("sbuf", [128, 256], X4), "hp": ("sbuf", [128, 256], "uint8"),
    "ps": ("psum", [128, 4096], "float32"),
}
_RANK_SEMS = (["la", "w0", "w1", "qs", "qa", "qb0", "qb1", "tv", "ta", "tb", "qq0", "qq1", "e0", "e2", "e3", "sent", "ow", "yv", "st"]
              + ["lb%d" % s for s in range(4)] + ["lg%d" % s for s in range(4)]
              + ["u%d" % s for s in range(4)] + ["qu%d" % s for s in range(4)]
              + ["z%d%d" % (k, i) for k in range(2) for i in range(2)]
              + ["d%d%d" % (k, b) for k in range(2) for b in range(4)]
              + ["r%d%d" % (k, b) for k in range(2) for b in range(4)]
              + ["y%d" % b for b in range(4)]
              + ["inq%d" % r for r in range(4)] + ["inu%d" % r for r in range(4)])
SEMAPHORES = _RANK_SEMS + ["hq", "hu", "hs"]

C = float(np.float32(0.019))
Q0, Q1, U0, U1, Q2, Q3, U3, U2 = [128 * k for k in range(8)]


def bits(mask):
    return [1 << k for k in range(mask.bit_length()) if mask >> k & 1]


def slots_of(r, T, topo):
    me = T.cores[r]
    far = [d for d in range(len(T.cores)) if d != r and not topo.may_write(me, T.cores[d])]
    near = [d for d in range(len(T.cores)) if d != r and topo.may_write(me, T.cores[d])]
    if r > near[0]:
        far = far[::-1]
    return far + [r] + near


def helpers_of(r, T, topo):
    me, far = T.cores[r], T.cores[slots_of(r, T, topo)[0]]
    chip = [c for c in range(256) if c != me and topo.host(c) == topo.host(me) and topo.chip(c) == topo.chip(me) and topo.may_write(c, far)]
    near = [c for c in chip if topo.die(c) == topo.die(me)]
    away = [c for c in chip if topo.die(c) != topo.die(me)]
    return near[:2], away[:2]


def codes(buf, lo, n=128):
    return buf[:, lo:lo + n].bitcast(dt.uint8)


def helper_program(g, core, T, topo):
    for r in range(len(T.cores)):
        for slot, pair in enumerate(helpers_of(r, T, topo)):
            if core not in pair:
                continue
            dst = T.cores[slots_of(r, T, topo)[slot]]
            rid, pid = topo.addr(dst, core)
            m = topo.mask(core, dst)
            hop = len(bits(topo.mask(T.cores[r], core)))
            for k, (sem, need, land) in enumerate((("hq", hop // 2, "inq%d" % r), ("hu", hop, "inu%d" % r))):
                g.wait_ge(T.sem[sem], need)
                if core == pair[0]:
                    g.remote_dma(codes(T.lc, 256 * r + 128 * k), codes(T.hc, 128 * k), T.sem[land], T.sem.hs, pid, rid, m)
                else:
                    o, i = 256 * r + 128 * k, 128 * k
                    g.remote_dma(T.lp[:, o:o + 128], T.hp[:, i:i + 128], T.sem[land], T.sem.hs, pid, rid, m)
            g.wait_ge(T.sem.hs, 2 * len(bits(m)))


def rank_program(g, core, T, topo):
    rank = T.rank_of(core)
    if rank is None:
        helper_program(g, core, T, topo)
        return
    S = T.sem
    order = slots_of(rank, T, topo)
    relays = helpers_of(rank, T, topo)
    v, a, t = g.vector, g.scalar, g.tensor
    relu = ActivationFunctionType.Relu

    def bank(k, lo, n):
        return T.ps[:, 512 * k + lo:512 * k + lo + n]

    g.sync.dma_start(T.ab[:], T.a[:]).then_inc(S.la, 16)
    for s in range(4):
        q = a if s < 2 else g.sync
        c = order[s]
        q.dma_start(T.bb[:, 512 * s:512 * s + 512], T.b[:, 512 * c:512 * c + 512]).then_inc(S["lb%d" % s], 16)
    for s in (0, 1, 3, 2):
        c = order[s]
        g.sync.dma_start(T.gb[:, 512 * s:512 * s + 512], T.gr[:, 512 * c:512 * c + 512]).then_inc(S["lg%d" % s], 16)

    def quant(oc, op, lo, n, src, sem):
        v.quantize_mx(oc[:, lo:lo + n], op[:, lo:lo + n], src).then_inc(S[sem], 1)

    v.memset(T.w[:], 0.0).then_inc(S.w0, 1)
    v.wait_ge(S.w1, 1)
    for b in range(4):
        quant(T.sc, T.sp, 128 * b, 128, T.w[:, 3 - b:3 - b + 512], "qs")
    v.wait_ge(S.la, 16)
    quant(T.ac, T.ap, 0, 256, T.ab[:], "qa")
    for s in (0, 1):
        v.wait_ge(S["lb%d" % s], 16)
        quant(T.bc, T.bp, 128 * s, 128, T.bb[:, 512 * s:512 * s + 512], "qb0")
    v.wait_ge(S.z01, 1)
    v.tensor_scalar(T.h[:, 2:1024:4], bank(1, 0, 256), 0.0, C, AluOpType.max, AluOpType.mult).then_inc(S.tv, 1)
    v.tensor_scalar(T.h[:, 3:1024:4], bank(1, 0, 256), 0.0, -C, AluOpType.min, AluOpType.mult).then_inc(S.tv, 1)
    v.wait_ge(S.tv, 2)
    v.wait_ge(S.ta, 2)
    quant(T.tc, T.tp, Q0, 256, T.h[:, 0:1024], "qq0")
    v.wait_ge(S.lb2, 16)
    v.wait_ge(S.lb3, 16)
    quant(T.bc, T.bp, 256, 256, T.bb[:, 1024:2048], "qb1")

    def residual(s, n, k0, lo, sem):
        for b in range(4):
            v.wait_ge(S["r%d%d" % (s // 2, b)], 1)
            v.wait_ge(S["d%d%d" % (s // 2, b)], 1)
            e = T.rf[:, 512 * s + b:512 * s + 4 * n:4]
            v.tensor_tensor(e, e, bank(k0 + b, lo, n), AluOpType.subtract).then_inc(S[sem], 1)
        v.wait_ge(S[sem], 4)

    def second(s, col):
        lo, hi = 512 * s, 512 * s + 512
        v.wait_ge(S["lg%d" % s], 16)
        v.tensor_tensor(T.u[:, lo:hi], T.rf[:, lo:hi], T.gb[:, lo:hi], AluOpType.add).then_inc(S["u%d" % s], 1)
        v.wait_ge(S["u%d" % s], 1)
        quant(T.tc, T.tp, col, 128, T.u[:, lo:hi], "qu%d" % s)

    residual(0, 256, 4, 0, "e0")
    second(0, U0)
    second(1, U1)
    v.wait_ge(S.tb, 4)
    quant(T.tc, T.tp, Q2, 256, T.h[:, 1024:2048], "qq1")
    residual(3, 128, 0, 128, "e3")
    second(3, U3)
    residual(2, 128, 0, 0, "e2")
    second(2, U2)

    def relu_to(buf, half, b, k, sem):
        a.activation(buf[:, 1024 * half + b:1024 * half + 1024:4], bank(k, 0, 256), relu,
                     scale=C if b % 2 == 0 else -C).then_inc(S[sem], 1)

    a.wait_ge(S.z00, 1)
    for b in (0, 1):
        relu_to(T.h, 0, b, 0, "ta")
    for b in range(4):
        if b == 2:
            a.wait_ge(S.z01, 1)
            a.wait_ge(S.tv, 2)
        relu_to(T.rf, 0, b, b // 2, "r0%d" % b)
    a.wait_ge(S.z10, 1)
    a.wait_ge(S.z11, 1)
    for b in range(4):
        relu_to(T.h, 1, b, 2 + b // 2, "tb")
    for b in range(4):
        relu_to(T.rf, 1, b, 2 + b // 2, "r1%d" % b)
    a.wait_ge(S.e2, 4)
    for b in range(4):
        a.activation(T.ow[:, b:512:4], bank(b, 0, 128), ActivationFunctionType.Copy).then_inc(S.ow, 1)

    def mm(k, n, wc, wp, wlo, xc, xp, xlo, start, stop):
        return t.matmul_mx(bank(k, 0, n), wc[:, wlo:wlo + 128], wp[:, wlo:wlo + 128], xc[:, xlo:xlo + n], xp[:, xlo:xlo + n], start, stop)

    t.wait_ge(S.qa, 1)
    t.wait_ge(S.qb0, 2)
    for i in range(2):
        mm(i, 256, T.ac, T.ap, 128 * i, T.bc, T.bp, 0, True, True).then_inc(S["z0%d" % i], 1)
    t.wait_ge(S.qs, 4)
    t.wait_ge(S.qq0, 1)
    for b in range(4):
        mm(4 + b, 256, T.sc, T.sp, 128 * b, T.tc, T.tp, Q0, True, True).then_inc(S["d0%d" % b], 1)
    t.wait_ge(S.qb1, 1)
    for i in range(2):
        mm(2 + i, 256, T.ac, T.ap, 128 * i, T.bc, T.bp, 256, True, True).then_inc(S["z1%d" % i], 1)
    t.wait_ge(S.qq1, 1)
    for b in range(4):
        for x in range(4):
            t.wait_ge(S["r%d%d" % (b // 2, x)], 1)
        mm(b, 256, T.sc, T.sp, 128 * b, T.tc, T.tp, Q2, True, True).then_inc(S["d1%d" % b], 1)
    t.wait_ge(S.e0, 4)
    far0 = [r for r in range(4) if r != rank and slots_of(r, T, topo)[0] == rank][0]
    far1 = [r for r in range(4) if r != rank and slots_of(r, T, topo)[1] == rank][0]
    near = order[3]

    def add(xc, xp, lo, first=False, last=False):
        for b in range(4):
            m = mm(4 + b, 128, T.sc, T.sp, 128 * b, xc, xp, lo, first, last)
            if last:
                m.then_inc(S["y%d" % b], 1)

    landed = 2 * 8
    for r in (far0, far1, near):
        t.wait_ge(S["inq%d" % r], landed)
        add(T.lc, T.lp, 256 * r, first=r == far0)
    t.wait_ge(S.qu2, 1)
    add(T.tc, T.tp, U2)
    for r in (far0, near, far1):
        t.wait_ge(S["inu%d" % r], landed)
        add(T.lc, T.lp, 256 * r + 128, last=r == far1)

    v.wait_ge(S.ow, 4)
    for b in range(4):
        v.wait_ge(S["y%d" % b], 1)
        v.tensor_tensor(T.ys[:, b:512:4], bank(4 + b, 0, 128), T.ow[:, b:512:4], AluOpType.add).then_inc(S.yv, 1)
    g.sync.wait_ge(S.yv, 4)
    g.sync.dma_start(T.y[:], T.ys[:]).then_inc(S.st, 16)
    g.sync.wait_ge(S.st, 16)

    g.wait_ge(S.w0, 1)
    d = T.w[:, 3:515:4]
    g.affine_select(d, d, [[-1, 128]], AluOpType.not_equal, 1.0, 0, 1).then_inc(S.w1, 1)
    sent = [0]

    def send(dst, out, in_, sem):
        rid, pid = topo.addr(dst, core)
        m = topo.mask(core, dst)
        g.remote_dma(out, in_, sem, S.sent, pid, rid, m)
        sent[0] += len(bits(m))

    g.wait_ge(S.qq0, 1)
    for plane in (0, 1):
        tr = []
        for s in (0, 1):
            dst = relays[s][plane]
            rid, pid = topo.addr(dst, core)
            e = bits(topo.mask(core, dst))
            e = e[s * len(e) // 2:(s + 1) * len(e) // 2]
            sent[0] += len(e)
            tr.append(RemoteDMATransfer(
                dst_ids=[DstId(rid=rid, pnc=pid)], dma_engine_mask=sum(e), remote_sem=S.hq,
                src=T.tp[:, 128 * s:128 * s + 128] if plane else codes(T.tc, 128 * s),
                dst=T.hp[:, 0:128] if plane else codes(T.hc, 0)))
        g.remote_dma_fused(tr, local_sem=S.sent)
    for s, col in ((0, U0), (1, U1)):
        g.wait_ge(S["qu%d" % s], 1)
        send(relays[s][0], codes(T.hc, 128), codes(T.tc, col), S.hu)
        send(relays[s][1], T.hp[:, 128:256], T.tp[:, col:col + 128], S.hu)
    dst, lo = T.cores[near], 256 * rank
    for ready, col, sem in (("qq1", Q3, "inq%d" % rank), ("qu3", U3, "inu%d" % rank)):
        g.wait_ge(S[ready], 1)
        send(dst, codes(T.lc, lo), codes(T.tc, col), S[sem])
        send(dst, T.lp[:, lo:lo + 128], T.tp[:, col:col + 128], S[sem])
        lo += 128
    g.wait_ge(S.sent, sent[0])
